import numpy as np
import ml_dtypes


def mxq(x, axis, fmt="e4m3"):
    dtype, down = {"e4m3": (ml_dtypes.float8_e4m3fn, 7), "e5m2": (ml_dtypes.float8_e5m2, 14)}[fmt]
    v = np.moveaxis(np.asarray(x, np.float32).astype(ml_dtypes.bfloat16).astype(np.float64), axis, -1)
    blocks = v.reshape(v.shape[:-1] + (-1, 32))
    amax = np.abs(blocks).max(-1, keepdims=True)
    byte = np.maximum(np.where(amax > 0, np.frexp(amax)[1] - 1 + 127, 0) - down, 1)
    scale = np.exp2(byte - 127.0)
    codes = (blocks / scale).astype(np.float32).astype(dtype).astype(np.float64)
    return np.moveaxis((codes * scale).reshape(v.shape), -1, axis)


WIDE = False


def mx_kscale(k):
    if not WIDE:
        return np.ones(k)
    levels = np.array([10, -10, 5, -5, 0])
    if k % 512:
        return np.exp2(np.random.permutation(np.resize(levels, k // 32))).repeat(32)
    a = np.empty((k // 512, 16))
    for p in range(k // 512):
        a[p, :8] = np.random.permutation(np.resize(levels, 8))
        for g in range(8):
            far = levels[np.abs(levels - a[p, g]) >= 10]
            a[p, g + 8] = far[np.random.randint(len(far))]
    return np.exp2(a.ravel()).repeat(32)


def f64(x):
    return np.asarray(x).astype(np.float64)


def striped(idx):
    return np.tile(idx.reshape(-1, 16).T, (8, 1)).astype(np.uint16)


def unstriped(offs):
    return offs[:16].T.reshape(-1).astype(np.int64)


E2M1 = np.array([0.0, 0.5, 1.0, 1.5, 2.0, 3.0, 4.0, 6.0, -0.0, -0.5, -1.0, -1.5, -2.0, -3.0, -4.0, -6.0])


def pack_weight(w, fmt):
    k, n = w.shape
    w = f64(np.asarray(w, np.float32).astype(ml_dtypes.bfloat16)).reshape(k // 32, 32, n)
    amax = np.abs(w).max(1)
    if fmt == "e4m3":
        byte = np.frexp(amax)[1] - 1 + 127 - 7
    else:
        mant, ex = np.frexp(amax / 6.0)
        byte = np.where(mant > 0.5, ex, ex - 1) + 127
    byte = np.clip(np.where(amax > 0, byte, 1), 1, 254)
    scaled = (w * np.exp2(127.0 - byte)[:, None, :]).reshape(k, n).astype(np.float32)
    by_word = np.ascontiguousarray(scaled.reshape(k // 512, 128, 4, n).transpose(0, 1, 3, 2))
    if fmt == "e4m3":
        words = by_word.astype(ml_dtypes.float8_e4m3fn).view(np.uint8)
    else:
        c = by_word.astype(ml_dtypes.float4_e2m1fn).view(np.uint8) & 0xF
        words = (c[..., 0::2] | (c[..., 1::2] << 4)).reshape(k // 512, 128, 2 * n)
    return np.ascontiguousarray(words), np.ascontiguousarray(byte.astype(np.uint8).reshape(k // 512, 16, n))


def unpack_weight(words, scales, fmt):
    g, _, n = scales.shape
    words = np.ascontiguousarray(words).reshape(g, 128, n, -1)
    if fmt == "e4m3":
        vals = words.view(ml_dtypes.float8_e4m3fn).astype(np.float64)
    else:
        nib = np.empty((g, 128, n, 4), np.uint8)
        nib[..., 0::2] = words & 0xF
        nib[..., 1::2] = words >> 4
        vals = E2M1[nib]
    vals = vals * np.repeat(np.exp2(scales.astype(np.float64) - 127.0), 8, axis=1)[..., None]
    return vals.transpose(0, 1, 3, 2).reshape(g * 512, n)


def pack_table(v):
    words, scales = pack_weight(v, "e4m3")
    return np.concatenate([words.reshape(words.shape[0], -1), scales.reshape(scales.shape[0], -1)], axis=1)


def unpack_table(tab):
    g, t = tab.shape[0], tab.shape[1] // 528
    return unpack_weight(tab[:, :512 * t].reshape(g, 128, t, 4), tab[:, 512 * t:].reshape(g, 16, t), "e4m3")


def silu(v):
    return v / (1.0 + np.exp(-np.maximum(v, -700.0)))


K, M, T, S = 1024, 1024, 4096, 2048


def setup_inputs():
    n = np.random.standard_normal
    s = mx_kscale(K)[:, None]
    u = mx_kscale(512)[:, None]
    p_w4 = pack_weight(n((K, M)) / np.sqrt(K) / s, "e2m1")
    return {
        "tab": pack_table(n((K, T)) * s),
        "w4_words": p_w4[0],
        "w4_scales": p_w4[1],
        "down": (n((K, 512)) / np.sqrt(K) / s * u.T).astype(np.float32),
        "up": (0.5 * n((512, M)) / np.sqrt(512) / u).astype(np.float32),
        "b": (0.3 * n(1024)).astype(np.float32),
        "wgo": np.tile(np.random.uniform(0.5, 2.0, S), (128, 1)).astype(np.float32),
        "offs": striped(np.random.permutation(T)[:S]),
        "offs2": striped(np.random.permutation(T)[:S]),
    }


def reference(tab, w4_words, w4_scales, down, up, b, wgo, offs, offs2):
    tab_ = unpack_table(tab)[:, unstriped(offs)]
    w4_ = unpack_weight(w4_words, w4_scales, "e2m1")
    down_ = mxq(f64(down), 0, "e4m3")
    up_ = mxq(f64(up), 0, "e4m3")
    h_ = mxq(down_.T @ tab_, 0, "e4m3")
    y = w4_.T @ tab_ + up_.T @ h_
    out = np.zeros((M, T))
    out[:, unstriped(offs2)] = f64(wgo)[0] * (silu(y + f64(b)[:, None]))
    return out

@@ -1,0 +1,223 @@
+from contextlib import ExitStack
+
+import concourse.mybir as mybir
+from concourse.masks import make_identity
+
+K, M, T, S, R = 1024, 1024, 4096, 2048, 512
+FLOPS = 2 * K * R * S + 2 * K * M * S + 2 * R * M * S
+
+F32 = mybir.dt.float32
+BF16 = mybir.dt.bfloat16
+I32 = mybir.dt.int32
+U32 = mybir.dt.uint32
+U16 = mybir.dt.uint16
+U8 = mybir.dt.uint8
+FP8X4 = mybir.dt.float8_e4m3fn_x4
+FP4X4 = mybir.dt.float4_e2m1fn_x4
+SILU = mybir.ActivationFunctionType.Silu
+MULT = mybir.AluOpType.mult
+
+P = 128
+PACK = 4
+PASSES = K // (P * PACK)
+SLICE = 512
+SLICES = S // SLICE
+CHUNK = 128
+M_TILES = M // P
+PER_COLUMN = 16
+
+
+def tile_list_tabscat_l_silu_kernel(tc, tab, w4_words, w4_scales, down, up, b, wgo, offs, offs2, out):
+    nc = tc.nc
+    with ExitStack() as ctx:
+        lists = ctx.enter_context(tc.tile_pool(name="lists", bufs=1))
+        keep = ctx.enter_context(tc.tile_pool(name="keep", bufs=1))
+        raw = ctx.enter_context(tc.tile_pool(name="raw", bufs=2))
+        acts = ctx.enter_context(tc.tile_pool(name="acts", bufs=2))
+        h_psum = ctx.enter_context(tc.psum_pool(name="h_psum", bufs=4))
+        y_psum = ctx.enter_context(tc.psum_pool(name="y_psum", bufs=4))
+
+        tab_words = tab.bitcast(I32)
+        tab_scale_rows = tab_words[:, P * T :].rearrange("a (q w) -> a q w", q=16)
+
+        gather_list = lists.tile([P, S // PER_COLUMN], U16, name="gather_list")
+        scatter_list = lists.tile([P, S // PER_COLUMN], U16, name="scatter_list")
+        nc.sync.dma_start(gather_list[:], offs)
+
+        scale_table = keep.tile([P, T], U8, name="scale_table", align_bytes=64)
+        nc.vector.memset(scale_table[:].bitcast(I32), 0)
+        for q in range(4):
+            nc.sync.dma_start(scale_table[32 * q : 32 * q + 8, :].bitcast(I32), tab_scale_rows[:, 4 * q : 4 * q + 4, :])
+
+        down_raw = []
+        for a in range(PASSES):
+            rows = raw.tile([P, PACK, R], F32, name="rows", tag="raw")
+            nc.sync.dma_start(rows[:], down[512 * a : 512 * (a + 1), :].rearrange("(p j) c -> p j c", j=PACK))
+            down_raw.append(rows)
+        word_table = []
+        for a in range(PASSES):
+            words = keep.tile([P, T], I32, name="word_table%d" % a)
+            nc.sync.dma_start(words[:], tab_words[a, 0 : P * T].rearrange("(p t) -> p t", p=P))
+            word_table.append(words)
+        up_rows = up.rearrange("(p j) n -> p j n", j=PACK)
+        up_first = keep.tile([P, PACK, 2 * P], F32, name="up_first")
+        nc.sync.dma_start(up_first[:], up_rows[:, :, 0 : 2 * P])
+        w4 = keep.tile([P, PASSES, 2 * M], U8, name="w4", align_bytes=64)
+        nc.sync.dma_start(w4[:].bitcast(I32), w4_words.bitcast(I32).rearrange("a p w -> p a w"))
+        nc.sync.dma_start(scatter_list[:], offs2)
+
+        w4_sc = keep.tile([P, PASSES, M], U8, name="w4_sc", align_bytes=64)
+        nc.vector.memset(w4_sc[:].bitcast(I32), 0)
+        for q in range(4):
+            nc.sync.dma_start(
+                w4_sc[32 * q : 32 * q + 4].bitcast(I32),
+                w4_scales.bitcast(I32)[:, 4 * q : 4 * q + 4, :].rearrange("a r w -> r a w"),
+            )
+
+        identity = keep.tile([P, P], F32, name="identity")
+        make_identity(nc, identity[:])
+        bias_rows = keep.tile([P, P], F32, name="bias_rows")
+        nc.scalar.activation(bias_rows[:], identity[:], SILU, scale=0.0)
+        nc.sync.dma_start(bias_rows[0:M_TILES, :], b.rearrange("(m p) -> m p", p=P))
+        bias_turned = y_psum.tile([P, SLICE], F32, name="bias_turned", tag="y")
+        nc.tensor.transpose(bias_turned[:, 0:P], bias_rows[:], identity[:])
+        bias = keep.tile([P, M_TILES], F32, name="bias")
+        nc.scalar.copy(bias[:], bias_turned[:, 0:M_TILES])
+
+        scales_moved = keep.tile([P, S], U8, name="scales_moved", align_bytes=64)
+        nc.vector.memset(scales_moved[:].bitcast(I32), 0)
+
+        pages = [keep.tile([P, T], F32, name="page%d" % i) for i in range(2)]
+        for page in pages:
+            nc.vector.memset(page[:], 0.0)
+
+        scales = keep.tile([P, S], U8, name="scales", align_bytes=64)
+        nc.vector.tensor_copy(scales[:], scale_table[:].indirect(gather_list[:]))
+        for q in range(4):
+            nc.sync.dma_start(
+                scales_moved[32 * q : 32 * q + 4, :].bitcast(I32), scales[32 * q + 4 : 32 * q + 8, :].bitcast(I32)
+            )
+
+        down_codes, down_scales = [], []
+        for a in range(PASSES):
+            grouped = keep.tile([P, PACK * R], BF16, name="down_grouped%d" % a, align_bytes=64)
+            nc.scalar.copy(
+                grouped[:].rearrange("p (t m j) -> p m j t", t=PACK, j=PACK),
+                down_raw[a][:].rearrange("p j (m t) -> p m j t", t=PACK),
+            )
+            codes = keep.tile([P, R], U32, name="down_codes%d" % a, align_bytes=64)
+            plane = keep.tile([P, R], U8, name="down_scales%d" % a, align_bytes=64)
+            nc.vector.quantize_mx(codes[:].bitcast(FP8X4), plane[:], grouped[:])
+            down_codes.append(codes)
+            down_scales.append(plane)
+
+        picked = [keep.tile([P, S], U32, name="picked%d" % a, align_bytes=64) for a in range(PASSES)]
+        nc.vector.tensor_copy(picked[0][:], word_table[0][:].bitcast(U32).indirect(gather_list[:]))
+        for s in range(SLICES):
+            nc.vector.tensor_copy(
+                picked[1][:, s * SLICE : (s + 1) * SLICE],
+                word_table[1][:].bitcast(U32).indirect(gather_list[:, s * SLICE // PER_COLUMN : (s + 1) * SLICE // PER_COLUMN]),
+            )
+
+        up_second = raw.tile([P, PACK, 2 * P], F32, name="up_second", tag="raw")
+        nc.sync.dma_start(up_second[:], up_rows[:, :, 2 * P : 4 * P])
+        weight = raw.tile([P, S], F32, name="weight", tag="raw")
+        nc.sync.dma_start(weight[:], wgo)
+        up_third = raw.tile([P, PACK, 4 * P], F32, name="up_third", tag="raw")
+
+        up_grouped = keep.tile([P, PACK * M], BF16, name="up_grouped", align_bytes=64)
+        up_codes = keep.tile([P, M], U32, name="up_codes", align_bytes=64)
+        up_scales = keep.tile([P, M], U8, name="up_scales", align_bytes=64)
+
+        def quantise_up(source, first, width):
+            grouped = up_grouped[:, PACK * first : PACK * (first + width)]
+            nc.scalar.copy(
+                grouped.rearrange("p (c i j) -> p c j i", i=4, j=PACK),
+                source.rearrange("p j (c i) -> p c j i", i=4),
+            )
+            nc.vector.quantize_mx(
+                up_codes[:, first : first + width].bitcast(FP8X4), up_scales[:, first : first + width], grouped
+            )
+
+        h_grouped = keep.tile([P, PACK * S], BF16, name="h_grouped", align_bytes=64)
+        h_codes = keep.tile([P, S], U32, name="h_codes", align_bytes=64)
+        h_scales = keep.tile([P, S], U8, name="h_scales", align_bytes=64)
+
+        def make_h(s):
+            for c in range(SLICE // CHUNK):
+                first = s * SLICE + c * CHUNK
+                cols = slice(first, first + CHUNK)
+                bank = h_psum.tile([P, PACK, CHUNK], F32, name="h_bank", tag="h")
+                for a in range(PASSES):
+                    for t in range(PACK):
+                        nc.tensor.matmul_mx(
+                            bank[:, t, :],
+                            lhsT=down_codes[a][:, t * P : (t + 1) * P].bitcast(FP8X4),
+                            lhsT_scale=down_scales[a][:, t * P : (t + 1) * P],
+                            rhs=picked[a][:, cols].bitcast(FP8X4),
+                            rhs_scale=scales[4 * a : P, cols],
+                            start=(a == 0 and t == 0),
+                            stop=(a == PASSES - 1 and t == PACK - 1),
+                        )
+                nc.scalar.copy(
+                    h_grouped[:, PACK * first : PACK * (first + CHUNK)].rearrange("p (c i t) -> p c t i", i=4, t=PACK),
+                    bank[:].rearrange("p t (c i) -> p c t i", i=4),
+                )
+            cols = slice(s * SLICE, (s + 1) * SLICE)
+            nc.vector.quantize_mx(
+                h_codes[:, cols].bitcast(FP8X4), h_scales[:, cols], h_grouped[:, PACK * s * SLICE : PACK * (s + 1) * SLICE]
+            )
+
+        table_planes = [scales, scales_moved]
+
+        def place(m, act, first, last):
+            rows = slice(m * P, (m + 1) * P)
+            for s in range(first, last):
+                cols = slice(s * SLICE, (s + 1) * SLICE)
+                bank = y_psum.tile([P, SLICE], F32, name="y_bank", tag="y")
+                for a in range(PASSES):
+                    nc.tensor.matmul_mx(
+                        bank[:],
+                        lhsT=w4[:, a, 2 * m * P : 2 * (m + 1) * P].bitcast(FP4X4),
+                        lhsT_scale=w4_sc[:, a, rows],
+                        rhs=picked[a][:, cols].bitcast(FP8X4),
+                        rhs_scale=table_planes[a][:, cols],
+                        start=(a == 0),
+                        stop=False,
+                    )
+                nc.tensor.matmul_mx(
+                    bank[:],
+                    lhsT=up_codes[:, rows].bitcast(FP8X4),
+                    lhsT_scale=up_scales[:, rows],
+                    rhs=h_codes[:, cols].bitcast(FP8X4),
+                    rhs_scale=h_scales[:, cols],
+                    start=False,
+                    stop=True,
+                )
+                nc.scalar.activation(act[:, cols], bank[:], SILU, bias=bias[:, m : m + 1])
+            cols = slice(first * SLICE, last * SLICE)
+            places = scatter_list[:, first * SLICE // PER_COLUMN : last * SLICE // PER_COLUMN]
+            page = pages[m % 2]
+            nc.vector.tensor_tensor(page[:].indirect(places), act[:, cols], weight[:, cols], MULT)
+            if last == SLICES:
+                nc.sync.dma_start(out[rows, :], page[:])
+
+        act0 = acts.tile([P, S], F32, name="act0", tag="act")
+        act1 = acts.tile([P, S], F32, name="act1", tag="act")
+        quantise_up(up_first[:, :, 0:P], 0, P)
+        make_h(0)
+        place(0, act0, 0, 1)
+        quantise_up(up_first[:, :, P : 2 * P], P, P)
+        make_h(1)
+        make_h(2)
+        place(1, act1, 0, 1)
+        make_h(3)
+        quantise_up(up_second[:], 2 * P, 2 * P)
+        nc.sync.dma_start(up_third[:], up_rows[:, :, 4 * P : 8 * P])
+        place(0, act0, 1, 2)
+        place(0, act0, 2, SLICES)
+        quantise_up(up_third[:], 4 * P, 4 * P)
+        place(1, act1, 1, SLICES)
+        for m in range(2, M_TILES):
+            act = acts.tile([P, S], F32, name="act", tag="act")
+            place(m, act, 0, SLICES)

@@ -33,191 +33,211 @@ def tile_list_tabscat_l_silu_kernel(tc, tab, w4_words, w4_scales, down, up, b, w
         lists = ctx.enter_context(tc.tile_pool(name="lists", bufs=1))
         keep = ctx.enter_context(tc.tile_pool(name="keep", bufs=1))
         raw = ctx.enter_context(tc.tile_pool(name="raw", bufs=2))
+        ring = ctx.enter_context(tc.tile_pool(name="ring", bufs=3))
         acts = ctx.enter_context(tc.tile_pool(name="acts", bufs=2))
-        h_psum = ctx.enter_context(tc.psum_pool(name="h_psum", bufs=4))
-        y_psum = ctx.enter_context(tc.psum_pool(name="y_psum", bufs=4))
+        psum = ctx.enter_context(tc.psum_pool(name="psum", bufs=4))
 
         tab_words = tab.bitcast(I32)
         tab_scale_rows = tab_words[:, P * T :].rearrange("a (q w) -> a q w", q=16)
+        word_rows = [tab_words[a, 0 : P * T].rearrange("(p t) -> p t", p=P) for a in range(PASSES)]
+        down_rows = down.rearrange("(a p j) c -> a p j c", p=P, j=PACK)
+        up_rows = up.rearrange("(p j) n -> p j n", j=PACK)
 
         gather_list = lists.tile([P, S // PER_COLUMN], U16, name="gather_list")
         scatter_list = lists.tile([P, S // PER_COLUMN], U16, name="scatter_list")
+        scale_table = keep.tile([P, T], U8, name="scale_table", tag="scale_table", align_bytes=64)
+        bias_rows = keep.tile([P, P], F32, name="bias_rows")
+        nc.gpsimd.memset(scale_table[:].bitcast(I32), 0)
+        nc.gpsimd.memset(bias_rows[0:64, :], 0.0)
         nc.sync.dma_start(gather_list[:], offs)
-
-        scale_table = keep.tile([P, T], U8, name="scale_table", align_bytes=64)
-        nc.vector.memset(scale_table[:].bitcast(I32), 0)
+        nc.sync.dma_start(scatter_list[:], offs2)
+        words0 = keep.tile([P, T], I32, name="words0", tag="words0", align_bytes=64)
+        for cols in (slice(0, T // 8), slice(T // 8, T // 4)):
+            nc.sync.dma_start(words0[:, cols], word_rows[0][:, cols])
         for q in range(4):
             nc.sync.dma_start(scale_table[32 * q : 32 * q + 8, :].bitcast(I32), tab_scale_rows[:, 4 * q : 4 * q + 4, :])
-
-        down_raw = []
+        nc.sync.dma_start(words0[:, T // 4 :], word_rows[0][:, T // 4 :])
+        nc.sync.dma_start(bias_rows[0:M_TILES, :], b.rearrange("(m p) -> m p", p=P))
+        down_raw = [raw.tile([P, PACK, R], F32, name="down_raw", tag="raw", align_bytes=64) for a in range(PASSES)]
         for a in range(PASSES):
-            rows = raw.tile([P, PACK, R], F32, name="rows", tag="raw")
-            nc.sync.dma_start(rows[:], down[512 * a : 512 * (a + 1), :].rearrange("(p j) c -> p j c", j=PACK))
-            down_raw.append(rows)
-        word_table = []
-        for a in range(PASSES):
-            words = keep.tile([P, T], I32, name="word_table%d" % a)
-            nc.sync.dma_start(words[:], tab_words[a, 0 : P * T].rearrange("(p t) -> p t", p=P))
-            word_table.append(words)
-        up_rows = up.rearrange("(p j) n -> p j n", j=PACK)
+            nc.sync.dma_start(down_raw[a][:], down_rows[a])
+        words1 = keep.tile([P, T], I32, name="words1", tag="words1")
+        nc.sync.dma_start(words1[:], word_rows[1])
         up_first = keep.tile([P, PACK, 2 * P], F32, name="up_first")
         nc.sync.dma_start(up_first[:], up_rows[:, :, 0 : 2 * P])
         w4 = keep.tile([P, PASSES, 2 * M], U8, name="w4", align_bytes=64)
         nc.sync.dma_start(w4[:].bitcast(I32), w4_words.bitcast(I32).rearrange("a p w -> p a w"))
-        nc.sync.dma_start(scatter_list[:], offs2)
 
         w4_sc = keep.tile([P, PASSES, M], U8, name="w4_sc", align_bytes=64)
-        nc.vector.memset(w4_sc[:].bitcast(I32), 0)
-        for q in range(4):
-            nc.sync.dma_start(
-                w4_sc[32 * q : 32 * q + 4].bitcast(I32),
-                w4_scales.bitcast(I32)[:, 4 * q : 4 * q + 4, :].rearrange("a r w -> r a w"),
-            )
+        nc.gpsimd.memset(w4_sc[:].bitcast(I32), 0)
+        w4_scale_rows = w4_scales.bitcast(I32).rearrange("a (q r) w -> r q a w", r=4)
+        for r in range(4):
+            nc.sync.dma_start(w4_sc[r:P:32].bitcast(I32), w4_scale_rows[r])
 
         identity = keep.tile([P, P], F32, name="identity")
         make_identity(nc, identity[:])
-        bias_rows = keep.tile([P, P], F32, name="bias_rows")
-        nc.scalar.activation(bias_rows[:], identity[:], SILU, scale=0.0)
-        nc.sync.dma_start(bias_rows[0:M_TILES, :], b.rearrange("(m p) -> m p", p=P))
-        bias_turned = y_psum.tile([P, SLICE], F32, name="bias_turned", tag="y")
-        nc.tensor.transpose(bias_turned[:, 0:P], bias_rows[:], identity[:])
+        nc.scalar.activation(bias_rows[64:P, :], identity[64:P, :], SILU, scale=0.0)
+        bias_turned = psum.tile([P, P], F32, name="bias_turned", tag="ring_b")
+        nc.tensor.transpose(bias_turned[:], bias_rows[:], identity[:])
         bias = keep.tile([P, M_TILES], F32, name="bias")
         nc.scalar.copy(bias[:], bias_turned[:, 0:M_TILES])
 
-        scales_moved = keep.tile([P, S], U8, name="scales_moved", align_bytes=64)
-        nc.vector.memset(scales_moved[:].bitcast(I32), 0)
-
         pages = [keep.tile([P, T], F32, name="page%d" % i) for i in range(2)]
-        for page in pages:
-            nc.vector.memset(page[:], 0.0)
+        for i in range(4):
+            nc.vector.memset(pages[0][:, i * 1024 : (i + 1) * 1024], 0.0)
+            nc.gpsimd.memset(pages[1][:, i * 1024 : (i + 1) * 1024], 0.0)
 
         scales = keep.tile([P, S], U8, name="scales", align_bytes=64)
         nc.vector.tensor_copy(scales[:], scale_table[:].indirect(gather_list[:]))
-        for q in range(4):
-            nc.sync.dma_start(
-                scales_moved[32 * q : 32 * q + 4, :].bitcast(I32), scales[32 * q + 4 : 32 * q + 8, :].bitcast(I32)
-            )
+        picked0 = keep.tile([P, S], U32, name="picked0", tag="scale_table", align_bytes=64)
+        nc.vector.tensor_copy(picked0[:], words0[:].bitcast(U32).indirect(gather_list[:]))
 
-        down_codes, down_scales = [], []
+        down_grouped = keep.tile([P, PASSES * PACK * R], BF16, name="down_grouped", tag="down_grouped", align_bytes=64)
         for a in range(PASSES):
-            grouped = keep.tile([P, PACK * R], BF16, name="down_grouped%d" % a, align_bytes=64)
             nc.scalar.copy(
-                grouped[:].rearrange("p (t m j) -> p m j t", t=PACK, j=PACK),
+                down_grouped[:, a * PACK * R : (a + 1) * PACK * R].rearrange("p (t m j) -> p m j t", t=PACK, j=PACK),
                 down_raw[a][:].rearrange("p j (m t) -> p m j t", t=PACK),
             )
-            codes = keep.tile([P, R], U32, name="down_codes%d" % a, align_bytes=64)
-            plane = keep.tile([P, R], U8, name="down_scales%d" % a, align_bytes=64)
-            nc.vector.quantize_mx(codes[:].bitcast(FP8X4), plane[:], grouped[:])
-            down_codes.append(codes)
-            down_scales.append(plane)
-
-        picked = [keep.tile([P, S], U32, name="picked%d" % a, align_bytes=64) for a in range(PASSES)]
-        nc.vector.tensor_copy(picked[0][:], word_table[0][:].bitcast(U32).indirect(gather_list[:]))
-        for s in range(SLICES):
-            nc.vector.tensor_copy(
-                picked[1][:, s * SLICE : (s + 1) * SLICE],
-                word_table[1][:].bitcast(U32).indirect(gather_list[:, s * SLICE // PER_COLUMN : (s + 1) * SLICE // PER_COLUMN]),
+        down_codes = keep.tile([P, PASSES * R], U32, name="down_codes", tag="words0", align_bytes=64)
+        down_scales = keep.tile([P, PASSES * R], U8, name="down_scales", align_bytes=64)
+        for a in range(PASSES):
+            cols = slice(a * R, (a + 1) * R)
+            nc.vector.quantize_mx(
+                down_codes[:, cols].bitcast(FP8X4), down_scales[:, cols], down_grouped[:, a * PACK * R : (a + 1) * PACK * R]
             )
 
-        up_second = raw.tile([P, PACK, 2 * P], F32, name="up_second", tag="raw")
-        nc.sync.dma_start(up_second[:], up_rows[:, :, 2 * P : 4 * P])
-        weight = raw.tile([P, S], F32, name="weight", tag="raw")
-        nc.sync.dma_start(weight[:], wgo)
-        up_third = raw.tile([P, PACK, 4 * P], F32, name="up_third", tag="raw")
+        def list_columns(index_list, first, last):
+            return index_list[:, first * SLICE // PER_COLUMN : last * SLICE // PER_COLUMN]
 
-        up_grouped = keep.tile([P, PACK * M], BF16, name="up_grouped", align_bytes=64)
+        picked1 = keep.tile([P, S - SLICE], U32, name="picked1", tag="down_grouped", align_bytes=64)
+        picked = [[picked0[:, s * SLICE : (s + 1) * SLICE] for s in range(SLICES)]]
+        picked.append([picked1[:, s * SLICE : (s + 1) * SLICE] for s in range(SLICES - 1)])
+
+        def gather_words1(s):
+            nc.vector.tensor_copy(picked[1][s], words1[:].bitcast(U32).indirect(list_columns(gather_list, s, s + 1)))
+
+        for s in range(SLICES - 1):
+            gather_words1(s)
+
+        weight = raw.tile([P, S], F32, name="weight", tag="raw", align_bytes=64)
+        nc.sync.dma_start(weight[:], wgo)
+        scales_moved = raw.tile([P, S], U8, name="scales_moved", tag="raw", align_bytes=64)
+        nc.gpsimd.memset(scales_moved[:].bitcast(I32), 0)
+        for r in range(4):
+            nc.scalar.dma_start(scales_moved[r:P:32, :].bitcast(I32), scales[4 + r : P : 32, :].bitcast(I32))
+
         up_codes = keep.tile([P, M], U32, name="up_codes", align_bytes=64)
         up_scales = keep.tile([P, M], U8, name="up_scales", align_bytes=64)
 
         def quantise_up(source, first, width):
-            grouped = up_grouped[:, PACK * first : PACK * (first + width)]
+            grouped = ring.tile([P, PACK * width], BF16, name="up_grouped", tag="ring", align_bytes=64)
             nc.scalar.copy(
-                grouped.rearrange("p (c i j) -> p c j i", i=4, j=PACK),
+                grouped[:].rearrange("p (c i j) -> p c j i", i=4, j=PACK),
                 source.rearrange("p j (c i) -> p c j i", i=4),
             )
             nc.vector.quantize_mx(
-                up_codes[:, first : first + width].bitcast(FP8X4), up_scales[:, first : first + width], grouped
+                up_codes[:, first : first + width].bitcast(FP8X4), up_scales[:, first : first + width], grouped[:]
             )
 
-        h_grouped = keep.tile([P, PACK * S], BF16, name="h_grouped", align_bytes=64)
         h_codes = keep.tile([P, S], U32, name="h_codes", align_bytes=64)
         h_scales = keep.tile([P, S], U8, name="h_scales", align_bytes=64)
 
-        def make_h(s):
-            for c in range(SLICE // CHUNK):
-                first = s * SLICE + c * CHUNK
-                cols = slice(first, first + CHUNK)
-                bank = h_psum.tile([P, PACK, CHUNK], F32, name="h_bank", tag="h")
-                for a in range(PASSES):
-                    for t in range(PACK):
-                        nc.tensor.matmul_mx(
-                            bank[:, t, :],
-                            lhsT=down_codes[a][:, t * P : (t + 1) * P].bitcast(FP8X4),
-                            lhsT_scale=down_scales[a][:, t * P : (t + 1) * P],
-                            rhs=picked[a][:, cols].bitcast(FP8X4),
-                            rhs_scale=scales[4 * a : P, cols],
-                            start=(a == 0 and t == 0),
-                            stop=(a == PASSES - 1 and t == PACK - 1),
-                        )
+        def make_h(s, grouped, bank_ring, quantise_width):
+            chunks = SLICE // CHUNK
+            banks = [psum.tile([P, PACK, CHUNK], F32, name="h_bank", tag=bank_ring) for c in range(chunks)]
+            steps = [(a, c) for c in range(chunks) for a in range(PASSES)]
+            for a, c in sorted(steps) if s == 0 else steps:
+                cols = slice(c * CHUNK, (c + 1) * CHUNK)
+                for t in range(PACK):
+                    channels = slice(a * R + t * P, a * R + (t + 1) * P)
+                    nc.tensor.matmul_mx(
+                        banks[c][:, t, :],
+                        lhsT=down_codes[:, channels].bitcast(FP8X4),
+                        lhsT_scale=down_scales[:, channels],
+                        rhs=picked[a][s][:, cols].bitcast(FP8X4),
+                        rhs_scale=scales[4 * a : P, s * SLICE + c * CHUNK : s * SLICE + (c + 1) * CHUNK],
+                        start=(a == 0 and t == 0),
+                        stop=(a == PASSES - 1 and t == PACK - 1),
+                    )
+            for c in range(chunks):
                 nc.scalar.copy(
-                    h_grouped[:, PACK * first : PACK * (first + CHUNK)].rearrange("p (c i t) -> p c t i", i=4, t=PACK),
-                    bank[:].rearrange("p t (c i) -> p c t i", i=4),
+                    grouped[:, PACK * c * CHUNK : PACK * (c + 1) * CHUNK].rearrange("p (c i t) -> p c t i", i=4, t=PACK),
+                    banks[c][:].rearrange("p t (c i) -> p c t i", i=4),
                 )
-            cols = slice(s * SLICE, (s + 1) * SLICE)
-            nc.vector.quantize_mx(
-                h_codes[:, cols].bitcast(FP8X4), h_scales[:, cols], h_grouped[:, PACK * s * SLICE : PACK * (s + 1) * SLICE]
-            )
+            for first in range(0, SLICE, quantise_width):
+                cols = slice(s * SLICE + first, s * SLICE + first + quantise_width)
+                nc.vector.quantize_mx(
+                    h_codes[:, cols].bitcast(FP8X4), h_scales[:, cols], grouped[:, PACK * first : PACK * (first + quantise_width)]
+                )
+
+        def make_h_in_ring(s, bank_ring):
+            grouped = ring.tile([P, PACK * SLICE], BF16, name="h_grouped", tag="ring", align_bytes=64)
+            make_h(s, grouped, bank_ring, SLICE)
 
         table_planes = [scales, scales_moved]
 
-        def place(m, act, first, last):
+        def project(m, act, s, bank_ring="ring_a", width=SLICE):
             rows = slice(m * P, (m + 1) * P)
-            for s in range(first, last):
-                cols = slice(s * SLICE, (s + 1) * SLICE)
-                bank = y_psum.tile([P, SLICE], F32, name="y_bank", tag="y")
-                for a in range(PASSES):
-                    nc.tensor.matmul_mx(
-                        bank[:],
-                        lhsT=w4[:, a, 2 * m * P : 2 * (m + 1) * P].bitcast(FP4X4),
-                        lhsT_scale=w4_sc[:, a, rows],
-                        rhs=picked[a][:, cols].bitcast(FP8X4),
-                        rhs_scale=table_planes[a][:, cols],
-                        start=(a == 0),
-                        stop=False,
-                    )
+            for first in range(0, SLICE, width):
+                cols = slice(s * SLICE + first, s * SLICE + first + width)
+                bank = psum.tile([P, width], F32, name="y_bank", tag=bank_ring)
                 nc.tensor.matmul_mx(
                     bank[:],
                     lhsT=up_codes[:, rows].bitcast(FP8X4),
                     lhsT_scale=up_scales[:, rows],
                     rhs=h_codes[:, cols].bitcast(FP8X4),
                     rhs_scale=h_scales[:, cols],
-                    start=False,
-                    stop=True,
+                    start=True,
+                    stop=False,
                 )
+                for a in range(PASSES):
+                    nc.tensor.matmul_mx(
+                        bank[:],
+                        lhsT=w4[:, a, 2 * m * P : 2 * (m + 1) * P].bitcast(FP4X4),
+                        lhsT_scale=w4_sc[:, a, rows],
+                        rhs=picked[a][s][:, first : first + width].bitcast(FP8X4),
+                        rhs_scale=table_planes[a][:, cols],
+                        start=False,
+                        stop=(a == PASSES - 1),
+                    )
                 nc.scalar.activation(act[:, cols], bank[:], SILU, bias=bias[:, m : m + 1])
+
+        def place(m, act, first, last):
+            rows = slice(m * P, (m + 1) * P)
             cols = slice(first * SLICE, last * SLICE)
-            places = scatter_list[:, first * SLICE // PER_COLUMN : last * SLICE // PER_COLUMN]
             page = pages[m % 2]
-            nc.vector.tensor_tensor(page[:].indirect(places), act[:, cols], weight[:, cols], MULT)
+            nc.vector.tensor_tensor(page[:].indirect(list_columns(scatter_list, first, last)), act[:, cols], weight[:, cols], MULT)
             if last == SLICES:
                 nc.sync.dma_start(out[rows, :], page[:])
 
         act0 = acts.tile([P, S], F32, name="act0", tag="act")
         act1 = acts.tile([P, S], F32, name="act1", tag="act")
-        quantise_up(up_first[:, :, 0:P], 0, P)
-        make_h(0)
+        quantise_up(up_first[:], 0, 2 * P)
+        h_first = keep.tile([P, PACK * SLICE], BF16, name="h_first", tag="h_first", align_bytes=64)
+        make_h(0, h_first, "ring_a", CHUNK)
+        picked_last = keep.tile([P, SLICE], U32, name="picked_last", tag="h_first", align_bytes=64)
+        picked[1].append(picked_last[:])
+        gather_words1(SLICES - 1)
+        up_rest = keep.tile([P, PACK, M - 2 * P], F32, name="up_rest", tag="words1")
+        nc.sync.dma_start(up_rest[:], up_rows[:, :, 2 * P : M])
+
+        project(0, act0, 0, "ring_b", CHUNK)
         place(0, act0, 0, 1)
-        quantise_up(up_first[:, :, P : 2 * P], P, P)
-        make_h(1)
-        make_h(2)
+        make_h_in_ring(1, "ring_a")
+        make_h_in_ring(2, "ring_b")
+        project(1, act1, 0)
         place(1, act1, 0, 1)
-        make_h(3)
-        quantise_up(up_second[:], 2 * P, 2 * P)
-        nc.sync.dma_start(up_third[:], up_rows[:, :, 4 * P : 8 * P])
-        place(0, act0, 1, 2)
-        place(0, act0, 2, SLICES)
-        quantise_up(up_third[:], 4 * P, 4 * P)
+        make_h_in_ring(3, "ring_b")
+        for s in range(1, SLICES):
+            project(0, act0, s)
+            place(0, act0, s, s + 1)
+        quantise_up(up_rest[:, :, 0 : 2 * P], 2 * P, 2 * P)
+        quantise_up(up_rest[:, :, 2 * P :], 4 * P, 4 * P)
+        for s in range(1, SLICES):
+            project(1, act1, s)
         place(1, act1, 1, SLICES)
         for m in range(2, M_TILES):
             act = acts.tile([P, S], F32, name="act", tag="act")
+            for s in range(SLICES):
+                project(m, act, s)
             place(m, act, 0, SLICES)

from contextlib import ExitStack

import concourse.mybir as mybir
from concourse.masks import make_identity

K, M, T, S, R = 1024, 1024, 4096, 2048, 512
FLOPS = 2 * K * R * S + 2 * K * M * S + 2 * R * M * S

F32 = mybir.dt.float32
BF16 = mybir.dt.bfloat16
I32 = mybir.dt.int32
U32 = mybir.dt.uint32
U16 = mybir.dt.uint16
U8 = mybir.dt.uint8
FP8X4 = mybir.dt.float8_e4m3fn_x4
FP4X4 = mybir.dt.float4_e2m1fn_x4
SILU = mybir.ActivationFunctionType.Silu
MULT = mybir.AluOpType.mult

P = 128
PACK = 4
PASSES = K // (P * PACK)
SLICE = 512
SLICES = S // SLICE
CHUNK = 128
M_TILES = M // P
PER_COLUMN = 16


def tile_list_tabscat_l_silu_kernel(tc, tab, w4_words, w4_scales, down, up, b, wgo, offs, offs2, out):
    nc = tc.nc
    with ExitStack() as ctx:
        lists = ctx.enter_context(tc.tile_pool(name="lists", bufs=1))
        keep = ctx.enter_context(tc.tile_pool(name="keep", bufs=1))
        raw = ctx.enter_context(tc.tile_pool(name="raw", bufs=2))
        ring = ctx.enter_context(tc.tile_pool(name="ring", bufs=3))
        acts = ctx.enter_context(tc.tile_pool(name="acts", bufs=2))
        psum = ctx.enter_context(tc.psum_pool(name="psum", bufs=4))

        tab_words = tab.bitcast(I32)
        tab_scale_rows = tab_words[:, P * T :].rearrange("a (q w) -> a q w", q=16)
        word_rows = [tab_words[a, 0 : P * T].rearrange("(p t) -> p t", p=P) for a in range(PASSES)]
        down_rows = down.rearrange("(a p j) c -> a p j c", p=P, j=PACK)
        up_rows = up.rearrange("(p j) n -> p j n", j=PACK)

        gather_list = lists.tile([P, S // PER_COLUMN], U16, name="gather_list")
        scatter_list = lists.tile([P, S // PER_COLUMN], U16, name="scatter_list")
        scale_table = keep.tile([P, T], U8, name="scale_table", tag="scale_table", align_bytes=64)
        bias_rows = keep.tile([P, P], F32, name="bias_rows")
        nc.gpsimd.memset(scale_table[:].bitcast(I32), 0)
        nc.gpsimd.memset(bias_rows[0:64, :], 0.0)
        nc.sync.dma_start(gather_list[:], offs)
        nc.sync.dma_start(scatter_list[:], offs2)
        words0 = keep.tile([P, T], I32, name="words0", tag="words0", align_bytes=64)
        for cols in (slice(0, T // 8), slice(T // 8, T // 4)):
            nc.sync.dma_start(words0[:, cols], word_rows[0][:, cols])
        for q in range(4):
            nc.sync.dma_start(scale_table[32 * q : 32 * q + 8, :].bitcast(I32), tab_scale_rows[:, 4 * q : 4 * q + 4, :])
        nc.sync.dma_start(words0[:, T // 4 :], word_rows[0][:, T // 4 :])
        nc.sync.dma_start(bias_rows[0:M_TILES, :], b.rearrange("(m p) -> m p", p=P))
        down_raw = [raw.tile([P, PACK, R], F32, name="down_raw", tag="raw", align_bytes=64) for a in range(PASSES)]
        for a in range(PASSES):
            nc.sync.dma_start(down_raw[a][:], down_rows[a])
        words1 = keep.tile([P, T], I32, name="words1", tag="words1")
        nc.sync.dma_start(words1[:], word_rows[1])
        up_first = keep.tile([P, PACK, 2 * P], F32, name="up_first")
        nc.sync.dma_start(up_first[:], up_rows[:, :, 0 : 2 * P])
        w4 = keep.tile([P, PASSES, 2 * M], U8, name="w4", align_bytes=64)
        nc.sync.dma_start(w4[:].bitcast(I32), w4_words.bitcast(I32).rearrange("a p w -> p a w"))

        w4_sc = keep.tile([P, PASSES, M], U8, name="w4_sc", align_bytes=64)
        nc.gpsimd.memset(w4_sc[:].bitcast(I32), 0)
        w4_scale_rows = w4_scales.bitcast(I32).rearrange("a (q r) w -> r q a w", r=4)
        for r in range(4):
            nc.sync.dma_start(w4_sc[r:P:32].bitcast(I32), w4_scale_rows[r])

        identity = keep.tile([P, P], F32, name="identity")
        make_identity(nc, identity[:])
        nc.scalar.activation(bias_rows[64:P, :], identity[64:P, :], SILU, scale=0.0)
        bias_turned = psum.tile([P, P], F32, name="bias_turned", tag="ring_b")
        nc.tensor.transpose(bias_turned[:], bias_rows[:], identity[:])
        bias = keep.tile([P, M_TILES], F32, name="bias")
        nc.scalar.copy(bias[:], bias_turned[:, 0:M_TILES])

        pages = [keep.tile([P, T], F32, name="page%d" % i) for i in range(2)]
        for i in range(4):
            nc.vector.memset(pages[0][:, i * 1024 : (i + 1) * 1024], 0.0)
            nc.gpsimd.memset(pages[1][:, i * 1024 : (i + 1) * 1024], 0.0)

        scales = keep.tile([P, S], U8, name="scales", align_bytes=64)
        nc.vector.tensor_copy(scales[:], scale_table[:].indirect(gather_list[:]))
        picked0 = keep.tile([P, S], U32, name="picked0", tag="scale_table", align_bytes=64)
        nc.vector.tensor_copy(picked0[:], words0[:].bitcast(U32).indirect(gather_list[:]))

        down_grouped = keep.tile([P, PASSES * PACK * R], BF16, name="down_grouped", tag="down_grouped", align_bytes=64)
        for a in range(PASSES):
            nc.scalar.copy(
                down_grouped[:, a * PACK * R : (a + 1) * PACK * R].rearrange("p (t m j) -> p m j t", t=PACK, j=PACK),
                down_raw[a][:].rearrange("p j (m t) -> p m j t", t=PACK),
            )
        down_codes = keep.tile([P, PASSES * R], U32, name="down_codes", tag="words0", align_bytes=64)
        down_scales = keep.tile([P, PASSES * R], U8, name="down_scales", align_bytes=64)
        for a in range(PASSES):
            cols = slice(a * R, (a + 1) * R)
            nc.vector.quantize_mx(
                down_codes[:, cols].bitcast(FP8X4), down_scales[:, cols], down_grouped[:, a * PACK * R : (a + 1) * PACK * R]
            )

        def list_columns(index_list, first, last):
            return index_list[:, first * SLICE // PER_COLUMN : last * SLICE // PER_COLUMN]

        picked1 = keep.tile([P, S - SLICE], U32, name="picked1", tag="down_grouped", align_bytes=64)
        picked = [[picked0[:, s * SLICE : (s + 1) * SLICE] for s in range(SLICES)]]
        picked.append([picked1[:, s * SLICE : (s + 1) * SLICE] for s in range(SLICES - 1)])

        def gather_words1(s):
            nc.vector.tensor_copy(picked[1][s], words1[:].bitcast(U32).indirect(list_columns(gather_list, s, s + 1)))

        for s in range(SLICES - 1):
            gather_words1(s)

        weight = raw.tile([P, S], F32, name="weight", tag="raw", align_bytes=64)
        nc.sync.dma_start(weight[:], wgo)
        scales_moved = raw.tile([P, S], U8, name="scales_moved", tag="raw", align_bytes=64)
        nc.gpsimd.memset(scales_moved[:].bitcast(I32), 0)
        for r in range(4):
            nc.scalar.dma_start(scales_moved[r:P:32, :].bitcast(I32), scales[4 + r : P : 32, :].bitcast(I32))

        up_codes = keep.tile([P, M], U32, name="up_codes", align_bytes=64)
        up_scales = keep.tile([P, M], U8, name="up_scales", align_bytes=64)

        def quantise_up(source, first, width):
            grouped = ring.tile([P, PACK * width], BF16, name="up_grouped", tag="ring", align_bytes=64)
            nc.scalar.copy(
                grouped[:].rearrange("p (c i j) -> p c j i", i=4, j=PACK),
                source.rearrange("p j (c i) -> p c j i", i=4),
            )
            nc.vector.quantize_mx(
                up_codes[:, first : first + width].bitcast(FP8X4), up_scales[:, first : first + width], grouped[:]
            )

        h_codes = keep.tile([P, S], U32, name="h_codes", align_bytes=64)
        h_scales = keep.tile([P, S], U8, name="h_scales", align_bytes=64)

        def make_h(s, grouped, bank_ring, quantise_width):
            chunks = SLICE // CHUNK
            banks = [psum.tile([P, PACK, CHUNK], F32, name="h_bank", tag=bank_ring) for c in range(chunks)]
            steps = [(a, c) for c in range(chunks) for a in range(PASSES)]
            for a, c in sorted(steps) if s == 0 else steps:
                cols = slice(c * CHUNK, (c + 1) * CHUNK)
                for t in range(PACK):
                    channels = slice(a * R + t * P, a * R + (t + 1) * P)
                    nc.tensor.matmul_mx(
                        banks[c][:, t, :],
                        lhsT=down_codes[:, channels].bitcast(FP8X4),
                        lhsT_scale=down_scales[:, channels],
                        rhs=picked[a][s][:, cols].bitcast(FP8X4),
                        rhs_scale=scales[4 * a : P, s * SLICE + c * CHUNK : s * SLICE + (c + 1) * CHUNK],
                        start=(a == 0 and t == 0),
                        stop=(a == PASSES - 1 and t == PACK - 1),
                    )
            for c in range(chunks):
                nc.scalar.copy(
                    grouped[:, PACK * c * CHUNK : PACK * (c + 1) * CHUNK].rearrange("p (c i t) -> p c t i", i=4, t=PACK),
                    banks[c][:].rearrange("p t (c i) -> p c t i", i=4),
                )
            for first in range(0, SLICE, quantise_width):
                cols = slice(s * SLICE + first, s * SLICE + first + quantise_width)
                nc.vector.quantize_mx(
                    h_codes[:, cols].bitcast(FP8X4), h_scales[:, cols], grouped[:, PACK * first : PACK * (first + quantise_width)]
                )

        def make_h_in_ring(s, bank_ring):
            grouped = ring.tile([P, PACK * SLICE], BF16, name="h_grouped", tag="ring", align_bytes=64)
            make_h(s, grouped, bank_ring, SLICE)

        table_planes = [scales, scales_moved]

        def project(m, act, s, bank_ring="ring_a", width=SLICE):
            rows = slice(m * P, (m + 1) * P)
            for first in range(0, SLICE, width):
                cols = slice(s * SLICE + first, s * SLICE + first + width)
                bank = psum.tile([P, width], F32, name="y_bank", tag=bank_ring)
                nc.tensor.matmul_mx(
                    bank[:],
                    lhsT=up_codes[:, rows].bitcast(FP8X4),
                    lhsT_scale=up_scales[:, rows],
                    rhs=h_codes[:, cols].bitcast(FP8X4),
                    rhs_scale=h_scales[:, cols],
                    start=True,
                    stop=False,
                )
                for a in range(PASSES):
                    nc.tensor.matmul_mx(
                        bank[:],
                        lhsT=w4[:, a, 2 * m * P : 2 * (m + 1) * P].bitcast(FP4X4),
                        lhsT_scale=w4_sc[:, a, rows],
                        rhs=picked[a][s][:, first : first + width].bitcast(FP8X4),
                        rhs_scale=table_planes[a][:, cols],
                        start=False,
                        stop=(a == PASSES - 1),
                    )
                nc.scalar.activation(act[:, cols], bank[:], SILU, bias=bias[:, m : m + 1])

        def place(m, act, first, last):
            rows = slice(m * P, (m + 1) * P)
            cols = slice(first * SLICE, last * SLICE)
            page = pages[m % 2]
            nc.vector.tensor_tensor(page[:].indirect(list_columns(scatter_list, first, last)), act[:, cols], weight[:, cols], MULT)
            if last == SLICES:
                nc.sync.dma_start(out[rows, :], page[:])

        act0 = acts.tile([P, S], F32, name="act0", tag="act")
        act1 = acts.tile([P, S], F32, name="act1", tag="act")
        quantise_up(up_first[:], 0, 2 * P)
        h_first = keep.tile([P, PACK * SLICE], BF16, name="h_first", tag="h_first", align_bytes=64)
        make_h(0, h_first, "ring_a", CHUNK)
        picked_last = keep.tile([P, SLICE], U32, name="picked_last", tag="h_first", align_bytes=64)
        picked[1].append(picked_last[:])
        gather_words1(SLICES - 1)
        up_rest = keep.tile([P, PACK, M - 2 * P], F32, name="up_rest", tag="words1")
        nc.sync.dma_start(up_rest[:], up_rows[:, :, 2 * P : M])

        project(0, act0, 0, "ring_b", CHUNK)
        place(0, act0, 0, 1)
        make_h_in_ring(1, "ring_a")
        make_h_in_ring(2, "ring_b")
        project(1, act1, 0)
        place(1, act1, 0, 1)
        make_h_in_ring(3, "ring_b")
        for s in range(1, SLICES):
            project(0, act0, s)
            place(0, act0, s, s + 1)
        quantise_up(up_rest[:, :, 0 : 2 * P], 2 * P, 2 * P)
        quantise_up(up_rest[:, :, 2 * P :], 4 * P, 4 * P)
        for s in range(1, SLICES):
            project(1, act1, s)
        place(1, act1, 1, SLICES)
        for m in range(2, M_TILES):
            act = acts.tile([P, S], F32, name="act", tag="act")
            for s in range(SLICES):
                project(m, act, s)
            place(m, act, 0, SLICES)
